import numpy as np
import ml_dtypes


def mxq(x, axis, fmt="e4m3"):
    dtype, down = {"e4m3": (ml_dtypes.float8_e4m3fn, 7), "e5m2": (ml_dtypes.float8_e5m2, 14)}[fmt]
    v = np.moveaxis(np.asarray(x, np.float32).astype(ml_dtypes.bfloat16).astype(np.float64), axis, -1)
    blocks = v.reshape(v.shape[:-1] + (-1, 32))
    amax = np.abs(blocks).max(-1, keepdims=True)
    byte = np.maximum(np.where(amax > 0, np.frexp(amax)[1] - 1 + 127, 0) - down, 1)
    scale = np.exp2(byte - 127.0)
    codes = (blocks / scale).astype(np.float32).astype(dtype).astype(np.float64)
    return np.moveaxis((codes * scale).reshape(v.shape), -1, axis)


WIDE = False


def mx_kscale(k):
    if not WIDE:
        return np.ones(k)
    levels = np.array([10, -10, 5, -5, 0])
    if k % 512:
        return np.exp2(np.random.permutation(np.resize(levels, k // 32))).repeat(32)
    a = np.empty((k // 512, 16))
    for p in range(k // 512):
        a[p, :8] = np.random.permutation(np.resize(levels, 8))
        for g in range(8):
            far = levels[np.abs(levels - a[p, g]) >= 10]
            a[p, g + 8] = far[np.random.randint(len(far))]
    return np.exp2(a.ravel()).repeat(32)


def f64(x):
    return np.asarray(x).astype(np.float64)


def striped(idx):
    return np.tile(idx.reshape(-1, 16).T, (8, 1)).astype(np.uint16)


def unstriped(offs):
    return offs[:16].T.reshape(-1).astype(np.int64)


E2M1 = np.array([0.0, 0.5, 1.0, 1.5, 2.0, 3.0, 4.0, 6.0, -0.0, -0.5, -1.0, -1.5, -2.0, -3.0, -4.0, -6.0])


def pack_weight(w, fmt):
    k, n = w.shape
    w = f64(np.asarray(w, np.float32).astype(ml_dtypes.bfloat16)).reshape(k // 32, 32, n)
    amax = np.abs(w).max(1)
    if fmt == "e4m3":
        byte = np.frexp(amax)[1] - 1 + 127 - 7
    else:
        mant, ex = np.frexp(amax / 6.0)
        byte = np.where(mant > 0.5, ex, ex - 1) + 127
    byte = np.clip(np.where(amax > 0, byte, 1), 1, 254)
    scaled = (w * np.exp2(127.0 - byte)[:, None, :]).reshape(k, n).astype(np.float32)
    by_word = np.ascontiguousarray(scaled.reshape(k // 512, 128, 4, n).transpose(0, 1, 3, 2))
    if fmt == "e4m3":
        words = by_word.astype(ml_dtypes.float8_e4m3fn).view(np.uint8)
    else:
        c = by_word.astype(ml_dtypes.float4_e2m1fn).view(np.uint8) & 0xF
        words = (c[..., 0::2] | (c[..., 1::2] << 4)).reshape(k // 512, 128, 2 * n)
    return np.ascontiguousarray(words), np.ascontiguousarray(byte.astype(np.uint8).reshape(k // 512, 16, n))


def unpack_weight(words, scales, fmt):
    g, _, n = scales.shape
    words = np.ascontiguousarray(words).reshape(g, 128, n, -1)
    if fmt == "e4m3":
        vals = words.view(ml_dtypes.float8_e4m3fn).astype(np.float64)
    else:
        nib = np.empty((g, 128, n, 4), np.uint8)
        nib[..., 0::2] = words & 0xF
        nib[..., 1::2] = words >> 4
        vals = E2M1[nib]
    vals = vals * np.repeat(np.exp2(scales.astype(np.float64) - 127.0), 8, axis=1)[..., None]
    return vals.transpose(0, 1, 3, 2).reshape(g * 512, n)


K, T, E, C, N = 512, 512, 12, 128, 512
TOP = 3


def by_expert(wq, xq):
    return np.concatenate([wq[e].T @ xq[:, e * C:(e + 1) * C] for e in range(E)], axis=1)


def setup_inputs():
    n = np.random.standard_normal
    s = mx_kscale(K)[:, None]
    deal = np.repeat(np.arange(E), C).reshape(TOP, T)[:, np.random.permutation(T)]
    deal = np.take_along_axis(deal, np.argsort(np.random.rand(TOP, T), axis=0), axis=0)
    for _ in range(8):
        s_, t_ = np.random.permutation(T).reshape(2, -1); r = np.random.randint(TOP, size=T // 2); x, y = deal[r, s_].copy(), deal[r, t_].copy()
        ok = ~((deal[:, s_] == y).any(0) | (deal[:, t_] == x).any(0)); deal[r[ok], s_[ok]] = y[ok]; deal[r[ok], t_[ok]] = x[ok]
    order = np.lexsort((np.random.rand(TOP * T), deal.reshape(-1)))
    slot_token = order % T; pos = np.empty(TOP * T, np.int64); pos[order] = np.arange(TOP * T); pos = pos.reshape(TOP, T)
    g = np.random.uniform(0.5, 1.5, (TOP, T)); g = g / g.sum(0)
    w = [pack_weight(m, "e2m1") for m in n((E + 1, K, N)) / np.sqrt(K) / s[None]]
    return {
        "xT": (n((K, T)) * s).astype(np.float32),
        "w_words": np.stack([m[0] for m in w]),
        "w_scales": np.stack([m[1] for m in w]),
        "gate": np.stack([np.tile(r, (N, 1)) for r in g]).astype(np.float32),
        "offs": striped(slot_token),
        "pos1": striped(pos[0]),
        "pos2": striped(pos[1]),
        "pos3": striped(pos[2]),
    }


def reference(xT, w_words, w_scales, gate, offs, pos1, pos2, pos3):
    idx = unstriped(offs)
    w = np.stack([unpack_weight(w_words[e], w_scales[e], "e2m1") for e in range(E + 1)])
    wq = w
    xs = mxq(f64(xT), 0, "e4m3")
    ys = wq[E].T @ xs
    xq = mxq(f64(xT)[:, idx], 0, "e4m3")
    y = by_expert(w, xq)
    return ys + sum(f64(gate[r]) * y[:, unstriped(p)] for r, p in enumerate((pos1, pos2, pos3)))

@@ -1,0 +1,187 @@
+from contextlib import ExitStack
+
+import concourse.mybir as mybir
+from concourse.masks import make_identity
+
+K, T, E, C, N = 512, 512, 12, 128, 512
+TOP = 3
+SLOTS = E * C
+FLOPS = 2 * K * N * (SLOTS + T)
+
+F32 = mybir.dt.float32
+BF16 = mybir.dt.bfloat16
+U32 = mybir.dt.uint32
+I32 = mybir.dt.int32
+U16 = mybir.dt.uint16
+U8 = mybir.dt.uint8
+FP8X4 = mybir.dt.float8_e4m3fn_x4
+FP4X4 = mybir.dt.float4_e2m1fn_x4
+MULT = mybir.AluOpType.mult
+ADD = mybir.AluOpType.add
+
+P = 128
+CHUNK = 256
+CHUNKS = SLOTS // CHUNK
+BANK = 512
+BLOCKS = N // P
+GROUP = BANK // C
+
+
+def tile_moe_shr_lin_none_kernel(tc, xT, w_words, w_scales, gate, offs, pos1, pos2, pos3, out):
+    nc = tc.nc
+    with ExitStack() as ctx:
+        keep = ctx.enter_context(tc.tile_pool(name="keep", bufs=1))
+        ring = ctx.enter_context(tc.tile_pool(name="ring", bufs=3))
+        psum = ctx.enter_context(tc.psum_pool(name="psum", bufs=4))
+
+        planes = keep.tile([P, E + 1, N], U8, name="planes", align_bytes=64)
+        nc.vector.memset(planes[:].rearrange("p e n -> p (e n)").bitcast(I32), 0)
+
+        x_rows = xT.rearrange("(p j) t -> p j t", j=4)
+        raw = [keep.tile([P, 2, T], F32, name="raw%d" % u) for u in range(2)]
+        slot_list = keep.tile([P, SLOTS // 16], U16, name="slot_list")
+        nc.sync.dma_start(raw[0][:], x_rows[:, 0:2, :])
+        nc.sync.dma_start(slot_list[:], offs)
+        nc.sync.dma_start(raw[1][:], x_rows[:, 2:4, :])
+        for r in range(4):
+            nc.sync.dma_start(
+                planes[r:P:32, :, :].bitcast(I32),
+                w_scales[:, 0, r:16:4, :].rearrange("e q n -> q e n").bitcast(I32),
+            )
+        words = []
+        for g0 in range(0, E + 1, GROUP):
+            count = min(GROUP, E + 1 - g0)
+            group_words = keep.tile([P, count, 2 * N], U8, name="words%d" % g0, align_bytes=64)
+            nc.sync.dma_start(
+                group_words[:].bitcast(I32),
+                w_words[g0 : g0 + count, 0].rearrange("e p b -> p e b").bitcast(I32),
+            )
+            words.append(group_words)
+        pos = []
+        for r, src in enumerate((pos1, pos2, pos3)):
+            pos_r = keep.tile([P, T // 16], U16, name="pos%d" % r)
+            nc.sync.dma_start(pos_r[:], src)
+            pos.append(pos_r)
+        gates = []
+        for r in range(TOP):
+            gate_r = keep.tile([P, T], F32, name="gate%d" % r)
+            nc.sync.dma_start(gate_r[:], gate[r, 0:P, :])
+            gates.append(gate_r)
+
+        identity = keep.tile([P, P], F32, name="identity")
+        make_identity(nc, identity[:])
+
+        pairs = keep.tile([P, 4 * T], BF16, name="pairs")
+        nc.vector.tensor_copy(
+            pairs[:, 0 : 2 * T].rearrange("p (c i d) -> p c d i", i=4, d=2),
+            raw[0][:].rearrange("p d (c i) -> p c d i", i=4),
+        )
+        nc.scalar.copy(pairs[:, 2 * T : 4 * T].rearrange("p (t d) -> p t d", d=2), raw[1][:].rearrange("p d t -> p t d"))
+        pair_words = pairs[:].bitcast(U32)
+
+        def weight(e, b):
+            lhsT = words[e // GROUP][:, e % GROUP, 2 * P * b : 2 * P * (b + 1)].bitcast(FP4X4)
+            return lhsT, planes[:, e, P * b : P * (b + 1)]
+
+        picked = {}
+        woven = [keep.tile([P, 4 * T], BF16, name="woven%d" % c, align_bytes=64) for c in range(CHUNKS)]
+        codes = [keep.tile([P, CHUNK], U32, name="codes%d" % c, align_bytes=64) for c in range(CHUNKS)]
+        scales = [keep.tile([P, CHUNK], U8, name="scales%d" % c, align_bytes=64) for c in range(CHUNKS)]
+
+        def gather(c, u):
+            if u == 0:
+                picked[c] = ring.tile([P, 2 * CHUNK], U32, name="picked")
+            cols = slice(c * CHUNK // 16, (c + 1) * CHUNK // 16)
+            nc.vector.tensor_copy(
+                picked[c][:, u * CHUNK : (u + 1) * CHUNK], pair_words[:, u * T : (u + 1) * T].indirect(slot_list[:, cols])
+            )
+
+        def quantise(c):
+            nc.scalar.copy(
+                woven[c][:, 0 : 4 * CHUNK].bitcast(U32).rearrange("p (s u) -> p s u", u=2),
+                picked[c][:].rearrange("p (u s) -> p s u", u=2),
+            )
+            nc.vector.quantize_mx(codes[c][:].bitcast(FP8X4), scales[c][:], woven[c][:, 0 : 4 * CHUNK])
+
+        y = [keep.tile([P, SLOTS], F32, name="y%d" % b) for b in range(BLOCKS)]
+
+        def experts(b, first, count):
+            bank = psum.tile([P, BANK], F32, name="bank")
+            for i in range(count):
+                e = first + i
+                c, cols = divmod(e * C, CHUNK)
+                lhsT, lhsT_scale = weight(e, b)
+                nc.tensor.matmul_mx(
+                    bank[:, i * C : (i + 1) * C], lhsT=lhsT, lhsT_scale=lhsT_scale,
+                    rhs=codes[c][:, cols : cols + C].bitcast(FP8X4), rhs_scale=scales[c][:, cols : cols + C],
+                    start=True, stop=True,
+                )
+            nc.scalar.copy(y[b][:, first * C : (first + count) * C], bank[:, 0 : count * C])
+
+        LEAD = 3
+        for c in range(LEAD):
+            gather(c, 0)
+        for c in range(LEAD):
+            gather(c, 1)
+        for c in range(CHUNKS):
+            quantise(c)
+            if c + LEAD < CHUNKS:
+                gather(c + LEAD, 0)
+                gather(c + LEAD, 1)
+            experts(0, 2 * c, 2)
+            if c % 2 == 1:
+                experts(1, 2 * c - 2, GROUP)
+
+        all_woven = woven[CHUNKS - 1]
+        nc.vector.tensor_copy(
+            all_woven[:].bitcast(U32).rearrange("p (t u) -> p t u", u=2), pair_words.rearrange("p (u t) -> p t u", u=2)
+        )
+        all_codes = keep.tile([P, T], U32, name="all_codes", align_bytes=64)
+        all_scales = keep.tile([P, T], U8, name="all_scales", align_bytes=64)
+        nc.vector.quantize_mx(all_codes[:].bitcast(FP8X4), all_scales[:], all_woven[:])
+
+        first = [keep.tile([P, T], F32, name="first%d" % b) for b in range(BLOCKS + 1)]
+        second = [keep.tile([P, T], F32, name="second%d" % b) for b in range(BLOCKS)]
+        partial = {}
+
+        def gated(dst, b, r):
+            nc.vector.tensor_tensor(dst[:], y[b][:].indirect(pos[r][:]), gates[r][:], MULT)
+
+        def add_two(b):
+            shared = psum.tile([P, BANK], F32, name="bank")
+            lhsT, lhsT_scale = weight(E, b)
+            nc.tensor.matmul_mx(shared[:], lhsT=lhsT, lhsT_scale=lhsT_scale, rhs=all_codes[:].bitcast(FP8X4),
+                                rhs_scale=all_scales[:], start=True, stop=True)
+            ys = ring.tile([P, T], F32, name="ys")
+            nc.scalar.copy(ys[:], shared[:])
+            turned = psum.tile([P, BANK], F32, name="turned", bufs=2)
+            terms = (ys, first[b], second[b])
+            for i, term in enumerate(terms):
+                for q in range(4):
+                    cols = slice(q * P, (q + 1) * P)
+                    nc.tensor.matmul(turned[:, cols], term[:, cols], identity[:], is_transpose=True,
+                                     start=(i == 0 and q == 0), stop=(i == 2 and q == 3))
+            summed = ring.tile([P, T], F32, name="summed")
+            nc.scalar.copy(summed[:], turned[:])
+            back = psum.tile([P, BANK], F32, name="back", bufs=2)
+            for q in range(4):
+                cols = slice(q * P, (q + 1) * P)
+                nc.tensor.transpose(back[:, cols], summed[:, cols], identity[:])
+            partial[b] = back
+
+        def finish(b):
+            gated(first[b + 1], b, 2)
+            result = ring.tile([P, T], F32, name="result")
+            nc.vector.tensor_tensor(result[:], partial[b][:], first[b + 1][:], ADD)
+            nc.sync.dma_start(out[b * P : (b + 1) * P, :], result[:])
+
+        for b in range(BLOCKS):
+            gated(first[b], b, 0)
+            gated(second[b], b, 1)
+            add_two(b)
+            if b + 2 < BLOCKS:
+                for g in range(E // GROUP):
+                    experts(b + 2, g * GROUP, GROUP)
+            if b > 0:
+                finish(b - 1)
+        finish(BLOCKS - 1)

@@ -20,8 +20,11 @@ MULT = mybir.AluOpType.mult
 ADD = mybir.AluOpType.add
 
 P = 128
-CHUNK = 256
-CHUNKS = SLOTS // CHUNK
+HALF = T // 2
+CAST_SPLIT = 352
+CHUNK_EXPERTS = (2, 2, 2, 2, 2, 1, 1)
+CHUNKS = len(CHUNK_EXPERTS)
+CHUNK_FIRST = tuple(sum(CHUNK_EXPERTS[:c]) for c in range(CHUNKS))
 BANK = 512
 BLOCKS = N // P
 GROUP = BANK // C
@@ -38,11 +41,17 @@ def tile_moe_shr_lin_none_kernel(tc, xT, w_words, w_scales, gate, offs, pos1, po
         nc.vector.memset(planes[:].rearrange("p e n -> p (e n)").bitcast(I32), 0)
 
         x_rows = xT.rearrange("(p j) t -> p j t", j=4)
-        raw = [keep.tile([P, 2, T], F32, name="raw%d" % u) for u in range(2)]
+        low = keep.tile([P, 2, T], F32, name="low")
+        high = keep.tile([P, 2, T], F32, name="high")
         slot_list = keep.tile([P, SLOTS // 16], U16, name="slot_list")
-        nc.sync.dma_start(raw[0][:], x_rows[:, 0:2, :])
+        nc.sync.dma_start(low[:], x_rows[:, 0:2, :])
         nc.sync.dma_start(slot_list[:], offs)
-        nc.sync.dma_start(raw[1][:], x_rows[:, 2:4, :])
+        nc.sync.dma_start(high[:], x_rows[:, 2:4, :])
+        pos = []
+        for r, src in enumerate((pos1, pos2, pos3)):
+            pos_r = keep.tile([P, T // 16], U16, name="pos%d" % r)
+            nc.sync.dma_start(pos_r[:], src)
+            pos.append(pos_r)
         for r in range(4):
             nc.sync.dma_start(
                 planes[r:P:32, :, :].bitcast(I32),
@@ -57,11 +66,6 @@ def tile_moe_shr_lin_none_kernel(tc, xT, w_words, w_scales, gate, offs, pos1, po
                 w_words[g0 : g0 + count, 0].rearrange("e p b -> p e b").bitcast(I32),
             )
             words.append(group_words)
-        pos = []
-        for r, src in enumerate((pos1, pos2, pos3)):
-            pos_r = keep.tile([P, T // 16], U16, name="pos%d" % r)
-            nc.sync.dma_start(pos_r[:], src)
-            pos.append(pos_r)
         gates = []
         for r in range(TOP):
             gate_r = keep.tile([P, T], F32, name="gate%d" % r)
@@ -73,50 +77,60 @@ def tile_moe_shr_lin_none_kernel(tc, xT, w_words, w_scales, gate, offs, pos1, po
 
         pairs = keep.tile([P, 4 * T], BF16, name="pairs")
         nc.vector.tensor_copy(
-            pairs[:, 0 : 2 * T].rearrange("p (c i d) -> p c d i", i=4, d=2),
-            raw[0][:].rearrange("p d (c i) -> p c d i", i=4),
+            pairs[:, 0 : 2 * CAST_SPLIT].rearrange("p (c i d) -> p c d i", i=4, d=2),
+            low[:, :, 0:CAST_SPLIT].rearrange("p d (c i) -> p c d i", i=4),
         )
-        nc.scalar.copy(pairs[:, 2 * T : 4 * T].rearrange("p (t d) -> p t d", d=2), raw[1][:].rearrange("p d t -> p t d"))
+        nc.scalar.copy(
+            pairs[:, 2 * CAST_SPLIT : 2 * T].rearrange("p (t d) -> p t d", d=2),
+            low[:, :, CAST_SPLIT:T].rearrange("p d t -> p t d"),
+        )
+        nc.scalar.copy(pairs[:, 2 * T : 4 * T].rearrange("p (t d) -> p t d", d=2), high[:].rearrange("p d t -> p t d"))
         pair_words = pairs[:].bitcast(U32)
+        all_woven = keep.tile([P, 4 * T], BF16, name="all_woven", align_bytes=64)
+        nc.scalar.copy(
+            all_woven[:].bitcast(U32).rearrange("p (t u) -> p t u", u=2), pair_words.rearrange("p (u t) -> p t u", u=2)
+        )
 
         def weight(e, b):
             lhsT = words[e // GROUP][:, e % GROUP, 2 * P * b : 2 * P * (b + 1)].bitcast(FP4X4)
             return lhsT, planes[:, e, P * b : P * (b + 1)]
 
         picked = {}
-        woven = [keep.tile([P, 4 * T], BF16, name="woven%d" % c, align_bytes=64) for c in range(CHUNKS)]
-        codes = [keep.tile([P, CHUNK], U32, name="codes%d" % c, align_bytes=64) for c in range(CHUNKS)]
-        scales = [keep.tile([P, CHUNK], U8, name="scales%d" % c, align_bytes=64) for c in range(CHUNKS)]
+        operand = {}
 
         def gather(c, u):
+            width = CHUNK_EXPERTS[c] * C
             if u == 0:
-                picked[c] = ring.tile([P, 2 * CHUNK], U32, name="picked")
-            cols = slice(c * CHUNK // 16, (c + 1) * CHUNK // 16)
+                picked[c] = ring.tile([P, 2 * width], U32, name="picked")
+            cols = slice(CHUNK_FIRST[c] * C // 16, (CHUNK_FIRST[c] * C + width) // 16)
             nc.vector.tensor_copy(
-                picked[c][:, u * CHUNK : (u + 1) * CHUNK], pair_words[:, u * T : (u + 1) * T].indirect(slot_list[:, cols])
+                picked[c][:, u * width : (u + 1) * width], pair_words[:, u * T : (u + 1) * T].indirect(slot_list[:, cols])
             )
 
         def quantise(c):
+            width = CHUNK_EXPERTS[c] * C
+            woven = keep.tile([P, 4 * width], BF16, name="woven%d" % c, align_bytes=64)
             nc.scalar.copy(
-                woven[c][:, 0 : 4 * CHUNK].bitcast(U32).rearrange("p (s u) -> p s u", u=2),
+                woven[:].bitcast(U32).rearrange("p (s u) -> p s u", u=2),
                 picked[c][:].rearrange("p (u s) -> p s u", u=2),
             )
-            nc.vector.quantize_mx(codes[c][:].bitcast(FP8X4), scales[c][:], woven[c][:, 0 : 4 * CHUNK])
+            codes = keep.tile([P, width], U32, name="codes%d" % c, align_bytes=64)
+            scales = keep.tile([P, width], U8, name="scales%d" % c, align_bytes=64)
+            nc.vector.quantize_mx(codes[:].bitcast(FP8X4), scales[:], woven[:])
+            for i in range(CHUNK_EXPERTS[c]):
+                cols = slice(i * C, (i + 1) * C)
+                operand[CHUNK_FIRST[c] + i] = (codes[:, cols].bitcast(FP8X4), scales[:, cols])
 
         y = [keep.tile([P, SLOTS], F32, name="y%d" % b) for b in range(BLOCKS)]
 
-        def experts(b, first, count):
+        def experts(b, first_expert, count):
             bank = psum.tile([P, BANK], F32, name="bank")
             for i in range(count):
-                e = first + i
-                c, cols = divmod(e * C, CHUNK)
-                lhsT, lhsT_scale = weight(e, b)
-                nc.tensor.matmul_mx(
-                    bank[:, i * C : (i + 1) * C], lhsT=lhsT, lhsT_scale=lhsT_scale,
-                    rhs=codes[c][:, cols : cols + C].bitcast(FP8X4), rhs_scale=scales[c][:, cols : cols + C],
-                    start=True, stop=True,
-                )
-            nc.scalar.copy(y[b][:, first * C : (first + count) * C], bank[:, 0 : count * C])
+                lhsT, lhsT_scale = weight(first_expert + i, b)
+                rhs, rhs_scale = operand[first_expert + i]
+                nc.tensor.matmul_mx(bank[:, i * C : (i + 1) * C], lhsT=lhsT, lhsT_scale=lhsT_scale,
+                                    rhs=rhs, rhs_scale=rhs_scale, start=True, stop=True)
+            nc.scalar.copy(y[b][:, first_expert * C : (first_expert + count) * C], bank[:, 0 : count * C])
 
         LEAD = 3
         for c in range(LEAD):
@@ -128,60 +142,71 @@ def tile_moe_shr_lin_none_kernel(tc, xT, w_words, w_scales, gate, offs, pos1, po
             if c + LEAD < CHUNKS:
                 gather(c + LEAD, 0)
                 gather(c + LEAD, 1)
-            experts(0, 2 * c, 2)
-            if c % 2 == 1:
-                experts(1, 2 * c - 2, GROUP)
+            experts(0, CHUNK_FIRST[c], CHUNK_EXPERTS[c])
+        for g in range(E // GROUP):
+            experts(1, g * GROUP, GROUP)
 
-        all_woven = woven[CHUNKS - 1]
-        nc.vector.tensor_copy(
-            all_woven[:].bitcast(U32).rearrange("p (t u) -> p t u", u=2), pair_words.rearrange("p (u t) -> p t u", u=2)
-        )
         all_codes = keep.tile([P, T], U32, name="all_codes", align_bytes=64)
-        all_scales = keep.tile([P, T], U8, name="all_scales", align_bytes=64)
+        all_scales = keep.tile([P, T], U8, name="all_scales", tag="woven%d" % (CHUNKS - 1), align_bytes=64)
         nc.vector.quantize_mx(all_codes[:].bitcast(FP8X4), all_scales[:], all_woven[:])
 
-        first = [keep.tile([P, T], F32, name="first%d" % b) for b in range(BLOCKS + 1)]
-        second = [keep.tile([P, T], F32, name="second%d" % b) for b in range(BLOCKS)]
-        partial = {}
+        products = [[keep.tile([P, T], F32, name="product%d_%d" % (b, r)) for r in range(TOP)] for b in range(BLOCKS)]
 
-        def gated(dst, b, r):
-            nc.vector.tensor_tensor(dst[:], y[b][:].indirect(pos[r][:]), gates[r][:], MULT)
+        def gated(dst, b, r, cols=slice(0, T)):
+            offsets = pos[r][:, cols.start // 16 : cols.stop // 16]
+            nc.vector.tensor_tensor(dst[:, cols], y[b][:].indirect(offsets), gates[r][:, cols], MULT)
 
-        def add_two(b):
-            shared = psum.tile([P, BANK], F32, name="bank")
+        def shared_expert(b):
+            bank = psum.tile([P, BANK], F32, name="bank")
             lhsT, lhsT_scale = weight(E, b)
-            nc.tensor.matmul_mx(shared[:], lhsT=lhsT, lhsT_scale=lhsT_scale, rhs=all_codes[:].bitcast(FP8X4),
+            nc.tensor.matmul_mx(bank[:], lhsT=lhsT, lhsT_scale=lhsT_scale, rhs=all_codes[:].bitcast(FP8X4),
                                 rhs_scale=all_scales[:], start=True, stop=True)
             ys = ring.tile([P, T], F32, name="ys")
-            nc.scalar.copy(ys[:], shared[:])
+            nc.scalar.copy(ys[:], bank[:])
+            return ys
+
+        def add_up(terms):
             turned = psum.tile([P, BANK], F32, name="turned", bufs=2)
-            terms = (ys, first[b], second[b])
             for i, term in enumerate(terms):
                 for q in range(4):
                     cols = slice(q * P, (q + 1) * P)
                     nc.tensor.matmul(turned[:, cols], term[:, cols], identity[:], is_transpose=True,
-                                     start=(i == 0 and q == 0), stop=(i == 2 and q == 3))
+                                     start=(i == 0 and q == 0), stop=(i == len(terms) - 1 and q == 3))
             summed = ring.tile([P, T], F32, name="summed")
             nc.scalar.copy(summed[:], turned[:])
             back = psum.tile([P, BANK], F32, name="back", bufs=2)
             for q in range(4):
                 cols = slice(q * P, (q + 1) * P)
                 nc.tensor.transpose(back[:, cols], summed[:, cols], identity[:])
-            partial[b] = back
+            return back
 
-        def finish(b):
-            gated(first[b + 1], b, 2)
+        for b in range(2):
+            ys = shared_expert(b)
+            for g in range(E // GROUP):
+                experts(b + 2, g * GROUP, GROUP)
+            for r in range(TOP):
+                gated(products[b][r], b, r)
+            back = add_up([ys] + products[b])
             result = ring.tile([P, T], F32, name="result")
-            nc.vector.tensor_tensor(result[:], partial[b][:], first[b + 1][:], ADD)
+            nc.scalar.copy(result[:], back[:])
             nc.sync.dma_start(out[b * P : (b + 1) * P, :], result[:])
 
-        for b in range(BLOCKS):
-            gated(first[b], b, 0)
-            gated(second[b], b, 1)
-            add_two(b)
-            if b + 2 < BLOCKS:
-                for g in range(E // GROUP):
-                    experts(b + 2, g * GROUP, GROUP)
-            if b > 0:
-                finish(b - 1)
-        finish(BLOCKS - 1)
+        partial = {}
+        for b in range(2, 4):
+            ys = shared_expert(b)
+            for r in range(2):
+                gated(products[b][r], b, r)
+            partial[b] = add_up([ys] + products[b][:2])
+
+        def finish(b, last, cols):
+            result = ring.tile([P, T], F32, name="result")
+            nc.vector.tensor_tensor(result[:, cols], partial[b][:, cols], last[:, cols], ADD)
+            nc.sync.dma_start(out[b * P : (b + 1) * P, cols], result[:, cols])
+
+        halves = (slice(0, HALF), slice(HALF, T))
+        gated(products[3][0], 2, 2)
+        gated(products[3][1], 3, 2, halves[0])
+        finish(2, products[3][0], slice(0, T))
+        gated(products[3][1], 3, 2, halves[1])
+        finish(3, products[3][1], halves[0])
+        finish(3, products[3][1], halves[1])

@@ -21,8 +21,9 @@ ADD = mybir.AluOpType.add
 
 P = 128
 HALF = T // 2
+WINDOW = 704
 CAST_SPLIT = 352
-CHUNK_EXPERTS = (2, 2, 2, 2, 2, 1, 1)
+CHUNK_EXPERTS = (4, 4, 2, 1, 1)
 CHUNKS = len(CHUNK_EXPERTS)
 CHUNK_FIRST = tuple(sum(CHUNK_EXPERTS[:c]) for c in range(CHUNKS))
 BANK = 512
@@ -75,7 +76,8 @@ def tile_moe_shr_lin_none_kernel(tc, xT, w_words, w_scales, gate, offs, pos1, po
         identity = keep.tile([P, P], F32, name="identity")
         make_identity(nc, identity[:])
 
-        pairs = keep.tile([P, 4 * T], BF16, name="pairs")
+        pairs = keep.tile([P, 4 * WINDOW], BF16, name="pairs")
+        nc.vector.memset(pairs[:].rearrange("p (u w) -> p u w", u=2)[:, :, 2 * T :], 0.0)
         nc.vector.tensor_copy(
             pairs[:, 0 : 2 * CAST_SPLIT].rearrange("p (c i d) -> p c d i", i=4, d=2),
             low[:, :, 0:CAST_SPLIT].rearrange("p d (c i) -> p c d i", i=4),
@@ -84,11 +86,11 @@ def tile_moe_shr_lin_none_kernel(tc, xT, w_words, w_scales, gate, offs, pos1, po
             pairs[:, 2 * CAST_SPLIT : 2 * T].rearrange("p (t d) -> p t d", d=2),
             low[:, :, CAST_SPLIT:T].rearrange("p d t -> p t d"),
         )
-        nc.scalar.copy(pairs[:, 2 * T : 4 * T].rearrange("p (t d) -> p t d", d=2), high[:].rearrange("p d t -> p t d"))
+        nc.scalar.copy(pairs[:, 2 * WINDOW : 2 * (WINDOW + T)].rearrange("p (t d) -> p t d", d=2), high[:].rearrange("p d t -> p t d"))
         pair_words = pairs[:].bitcast(U32)
         all_woven = keep.tile([P, 4 * T], BF16, name="all_woven", align_bytes=64)
         nc.scalar.copy(
-            all_woven[:].bitcast(U32).rearrange("p (t u) -> p t u", u=2), pair_words.rearrange("p (u t) -> p t u", u=2)
+            all_woven[:].bitcast(U32).rearrange("p (t u) -> p t u", u=2), pair_words.rearrange("p (u w) -> p w u", u=2)[:, 0:T, :]
         )
 
         def weight(e, b):
@@ -104,7 +106,8 @@ def tile_moe_shr_lin_none_kernel(tc, xT, w_words, w_scales, gate, offs, pos1, po
                 picked[c] = ring.tile([P, 2 * width], U32, name="picked")
             cols = slice(CHUNK_FIRST[c] * C // 16, (CHUNK_FIRST[c] * C + width) // 16)
             nc.vector.tensor_copy(
-                picked[c][:, u * width : (u + 1) * width], pair_words[:, u * T : (u + 1) * T].indirect(slot_list[:, cols])
+                picked[c][:, u * width : (u + 1) * width],
+                pair_words[:, u * WINDOW : (u + 1) * WINDOW].indirect(slot_list[:, cols]),
             )
 
         def quantise(c):
@@ -133,10 +136,12 @@ def tile_moe_shr_lin_none_kernel(tc, xT, w_words, w_scales, gate, offs, pos1, po
             nc.scalar.copy(y[b][:, first_expert * C : (first_expert + count) * C], bank[:, 0 : count * C])
 
         LEAD = 3
-        for c in range(LEAD):
+        for c in range(LEAD - 1):
             gather(c, 0)
-        for c in range(LEAD):
+        for c in range(LEAD - 1):
             gather(c, 1)
+        gather(LEAD - 1, 0)
+        gather(LEAD - 1, 1)
         for c in range(CHUNKS):
             quantise(c)
             if c + LEAD < CHUNKS:

from contextlib import ExitStack

import concourse.mybir as mybir
from concourse.masks import make_identity

K, T, E, C, N = 512, 512, 12, 128, 512
TOP = 3
SLOTS = E * C
FLOPS = 2 * K * N * (SLOTS + T)

F32 = mybir.dt.float32
BF16 = mybir.dt.bfloat16
U32 = mybir.dt.uint32
I32 = mybir.dt.int32
U16 = mybir.dt.uint16
U8 = mybir.dt.uint8
FP8X4 = mybir.dt.float8_e4m3fn_x4
FP4X4 = mybir.dt.float4_e2m1fn_x4
MULT = mybir.AluOpType.mult
ADD = mybir.AluOpType.add

P = 128
HALF = T // 2
WINDOW = 704
CAST_SPLIT = 352
CHUNK_EXPERTS = (4, 4, 2, 1, 1)
CHUNKS = len(CHUNK_EXPERTS)
CHUNK_FIRST = tuple(sum(CHUNK_EXPERTS[:c]) for c in range(CHUNKS))
BANK = 512
BLOCKS = N // P
GROUP = BANK // C


def tile_moe_shr_lin_none_kernel(tc, xT, w_words, w_scales, gate, offs, pos1, pos2, pos3, out):
    nc = tc.nc
    with ExitStack() as ctx:
        keep = ctx.enter_context(tc.tile_pool(name="keep", bufs=1))
        ring = ctx.enter_context(tc.tile_pool(name="ring", bufs=3))
        psum = ctx.enter_context(tc.psum_pool(name="psum", bufs=4))

        planes = keep.tile([P, E + 1, N], U8, name="planes", align_bytes=64)
        nc.vector.memset(planes[:].rearrange("p e n -> p (e n)").bitcast(I32), 0)

        x_rows = xT.rearrange("(p j) t -> p j t", j=4)
        low = keep.tile([P, 2, T], F32, name="low")
        high = keep.tile([P, 2, T], F32, name="high")
        slot_list = keep.tile([P, SLOTS // 16], U16, name="slot_list")
        nc.sync.dma_start(low[:], x_rows[:, 0:2, :])
        nc.sync.dma_start(slot_list[:], offs)
        nc.sync.dma_start(high[:], x_rows[:, 2:4, :])
        pos = []
        for r, src in enumerate((pos1, pos2, pos3)):
            pos_r = keep.tile([P, T // 16], U16, name="pos%d" % r)
            nc.sync.dma_start(pos_r[:], src)
            pos.append(pos_r)
        for r in range(4):
            nc.sync.dma_start(
                planes[r:P:32, :, :].bitcast(I32),
                w_scales[:, 0, r:16:4, :].rearrange("e q n -> q e n").bitcast(I32),
            )
        words = []
        for g0 in range(0, E + 1, GROUP):
            count = min(GROUP, E + 1 - g0)
            group_words = keep.tile([P, count, 2 * N], U8, name="words%d" % g0, align_bytes=64)
            nc.sync.dma_start(
                group_words[:].bitcast(I32),
                w_words[g0 : g0 + count, 0].rearrange("e p b -> p e b").bitcast(I32),
            )
            words.append(group_words)
        gates = []
        for r in range(TOP):
            gate_r = keep.tile([P, T], F32, name="gate%d" % r)
            nc.sync.dma_start(gate_r[:], gate[r, 0:P, :])
            gates.append(gate_r)

        identity = keep.tile([P, P], F32, name="identity")
        make_identity(nc, identity[:])

        pairs = keep.tile([P, 4 * WINDOW], BF16, name="pairs")
        nc.vector.memset(pairs[:].rearrange("p (u w) -> p u w", u=2)[:, :, 2 * T :], 0.0)
        nc.vector.tensor_copy(
            pairs[:, 0 : 2 * CAST_SPLIT].rearrange("p (c i d) -> p c d i", i=4, d=2),
            low[:, :, 0:CAST_SPLIT].rearrange("p d (c i) -> p c d i", i=4),
        )
        nc.scalar.copy(
            pairs[:, 2 * CAST_SPLIT : 2 * T].rearrange("p (t d) -> p t d", d=2),
            low[:, :, CAST_SPLIT:T].rearrange("p d t -> p t d"),
        )
        nc.scalar.copy(pairs[:, 2 * WINDOW : 2 * (WINDOW + T)].rearrange("p (t d) -> p t d", d=2), high[:].rearrange("p d t -> p t d"))
        pair_words = pairs[:].bitcast(U32)
        all_woven = keep.tile([P, 4 * T], BF16, name="all_woven", align_bytes=64)
        nc.scalar.copy(
            all_woven[:].bitcast(U32).rearrange("p (t u) -> p t u", u=2), pair_words.rearrange("p (u w) -> p w u", u=2)[:, 0:T, :]
        )

        def weight(e, b):
            lhsT = words[e // GROUP][:, e % GROUP, 2 * P * b : 2 * P * (b + 1)].bitcast(FP4X4)
            return lhsT, planes[:, e, P * b : P * (b + 1)]

        picked = {}
        operand = {}

        def gather(c, u):
            width = CHUNK_EXPERTS[c] * C
            if u == 0:
                picked[c] = ring.tile([P, 2 * width], U32, name="picked")
            cols = slice(CHUNK_FIRST[c] * C // 16, (CHUNK_FIRST[c] * C + width) // 16)
            nc.vector.tensor_copy(
                picked[c][:, u * width : (u + 1) * width],
                pair_words[:, u * WINDOW : (u + 1) * WINDOW].indirect(slot_list[:, cols]),
            )

        def quantise(c):
            width = CHUNK_EXPERTS[c] * C
            woven = keep.tile([P, 4 * width], BF16, name="woven%d" % c, align_bytes=64)
            nc.scalar.copy(
                woven[:].bitcast(U32).rearrange("p (s u) -> p s u", u=2),
                picked[c][:].rearrange("p (u s) -> p s u", u=2),
            )
            codes = keep.tile([P, width], U32, name="codes%d" % c, align_bytes=64)
            scales = keep.tile([P, width], U8, name="scales%d" % c, align_bytes=64)
            nc.vector.quantize_mx(codes[:].bitcast(FP8X4), scales[:], woven[:])
            for i in range(CHUNK_EXPERTS[c]):
                cols = slice(i * C, (i + 1) * C)
                operand[CHUNK_FIRST[c] + i] = (codes[:, cols].bitcast(FP8X4), scales[:, cols])

        y = [keep.tile([P, SLOTS], F32, name="y%d" % b) for b in range(BLOCKS)]

        def experts(b, first_expert, count):
            bank = psum.tile([P, BANK], F32, name="bank")
            for i in range(count):
                lhsT, lhsT_scale = weight(first_expert + i, b)
                rhs, rhs_scale = operand[first_expert + i]
                nc.tensor.matmul_mx(bank[:, i * C : (i + 1) * C], lhsT=lhsT, lhsT_scale=lhsT_scale,
                                    rhs=rhs, rhs_scale=rhs_scale, start=True, stop=True)
            nc.scalar.copy(y[b][:, first_expert * C : (first_expert + count) * C], bank[:, 0 : count * C])

        LEAD = 3
        for c in range(LEAD - 1):
            gather(c, 0)
        for c in range(LEAD - 1):
            gather(c, 1)
        gather(LEAD - 1, 0)
        gather(LEAD - 1, 1)
        for c in range(CHUNKS):
            quantise(c)
            if c + LEAD < CHUNKS:
                gather(c + LEAD, 0)
                gather(c + LEAD, 1)
            experts(0, CHUNK_FIRST[c], CHUNK_EXPERTS[c])
        for g in range(E // GROUP):
            experts(1, g * GROUP, GROUP)

        all_codes = keep.tile([P, T], U32, name="all_codes", align_bytes=64)
        all_scales = keep.tile([P, T], U8, name="all_scales", tag="woven%d" % (CHUNKS - 1), align_bytes=64)
        nc.vector.quantize_mx(all_codes[:].bitcast(FP8X4), all_scales[:], all_woven[:])

        products = [[keep.tile([P, T], F32, name="product%d_%d" % (b, r)) for r in range(TOP)] for b in range(BLOCKS)]

        def gated(dst, b, r, cols=slice(0, T)):
            offsets = pos[r][:, cols.start // 16 : cols.stop // 16]
            nc.vector.tensor_tensor(dst[:, cols], y[b][:].indirect(offsets), gates[r][:, cols], MULT)

        def shared_expert(b):
            bank = psum.tile([P, BANK], F32, name="bank")
            lhsT, lhsT_scale = weight(E, b)
            nc.tensor.matmul_mx(bank[:], lhsT=lhsT, lhsT_scale=lhsT_scale, rhs=all_codes[:].bitcast(FP8X4),
                                rhs_scale=all_scales[:], start=True, stop=True)
            ys = ring.tile([P, T], F32, name="ys")
            nc.scalar.copy(ys[:], bank[:])
            return ys

        def add_up(terms):
            turned = psum.tile([P, BANK], F32, name="turned", bufs=2)
            for i, term in enumerate(terms):
                for q in range(4):
                    cols = slice(q * P, (q + 1) * P)
                    nc.tensor.matmul(turned[:, cols], term[:, cols], identity[:], is_transpose=True,
                                     start=(i == 0 and q == 0), stop=(i == len(terms) - 1 and q == 3))
            summed = ring.tile([P, T], F32, name="summed")
            nc.scalar.copy(summed[:], turned[:])
            back = psum.tile([P, BANK], F32, name="back", bufs=2)
            for q in range(4):
                cols = slice(q * P, (q + 1) * P)
                nc.tensor.transpose(back[:, cols], summed[:, cols], identity[:])
            return back

        for b in range(2):
            ys = shared_expert(b)
            for g in range(E // GROUP):
                experts(b + 2, g * GROUP, GROUP)
            for r in range(TOP):
                gated(products[b][r], b, r)
            back = add_up([ys] + products[b])
            result = ring.tile([P, T], F32, name="result")
            nc.scalar.copy(result[:], back[:])
            nc.sync.dma_start(out[b * P : (b + 1) * P, :], result[:])

        partial = {}
        for b in range(2, 4):
            ys = shared_expert(b)
            for r in range(2):
                gated(products[b][r], b, r)
            partial[b] = add_up([ys] + products[b][:2])

        def finish(b, last, cols):
            result = ring.tile([P, T], F32, name="result")
            nc.vector.tensor_tensor(result[:, cols], partial[b][:, cols], last[:, cols], ADD)
            nc.sync.dma_start(out[b * P : (b + 1) * P, cols], result[:, cols])

        halves = (slice(0, HALF), slice(HALF, T))
        gated(products[3][0], 2, 2)
        gated(products[3][1], 3, 2, halves[0])
        finish(2, products[3][0], slice(0, T))
        gated(products[3][1], 3, 2, halves[1])
        finish(3, products[3][1], halves[0])
        finish(3, products[3][1], halves[1])
